import numpy as np
import ml_dtypes


def mxq(x, axis, fmt="e4m3"):
    dtype, down = {"e4m3": (ml_dtypes.float8_e4m3fn, 7), "e5m2": (ml_dtypes.float8_e5m2, 14)}[fmt]
    v = np.moveaxis(np.asarray(x, np.float32).astype(ml_dtypes.bfloat16).astype(np.float64), axis, -1)
    blocks = v.reshape(v.shape[:-1] + (-1, 32))
    amax = np.abs(blocks).max(-1, keepdims=True)
    byte = np.maximum(np.where(amax > 0, np.frexp(amax)[1] - 1 + 127, 0) - down, 1)
    scale = np.exp2(byte - 127.0)
    codes = (blocks / scale).astype(np.float32).astype(dtype).astype(np.float64)
    return np.moveaxis((codes * scale).reshape(v.shape), -1, axis)


WIDE = False


def mx_kscale(k):
    if not WIDE:
        return np.ones(k)
    levels = np.array([10, -10, 5, -5, 0])
    if k % 512:
        return np.exp2(np.random.permutation(np.resize(levels, k // 32))).repeat(32)
    a = np.empty((k // 512, 16))
    for p in range(k // 512):
        a[p, :8] = np.random.permutation(np.resize(levels, 8))
        for g in range(8):
            far = levels[np.abs(levels - a[p, g]) >= 10]
            a[p, g + 8] = far[np.random.randint(len(far))]
    return np.exp2(a.ravel()).repeat(32)


def f64(x):
    return np.asarray(x).astype(np.float64)


def striped(idx):
    return np.tile(idx.reshape(-1, 16).T, (8, 1)).astype(np.uint16)


def unstriped(offs):
    return offs[:16].T.reshape(-1).astype(np.int64)


E2M1 = np.array([0.0, 0.5, 1.0, 1.5, 2.0, 3.0, 4.0, 6.0, -0.0, -0.5, -1.0, -1.5, -2.0, -3.0, -4.0, -6.0])


def pack_weight(w, fmt):
    k, n = w.shape
    w = f64(np.asarray(w, np.float32).astype(ml_dtypes.bfloat16)).reshape(k // 32, 32, n)
    amax = np.abs(w).max(1)
    if fmt == "e4m3":
        byte = np.frexp(amax)[1] - 1 + 127 - 7
    else:
        mant, ex = np.frexp(amax / 6.0)
        byte = np.where(mant > 0.5, ex, ex - 1) + 127
    byte = np.clip(np.where(amax > 0, byte, 1), 1, 254)
    scaled = (w * np.exp2(127.0 - byte)[:, None, :]).reshape(k, n).astype(np.float32)
    by_word = np.ascontiguousarray(scaled.reshape(k // 512, 128, 4, n).transpose(0, 1, 3, 2))
    if fmt == "e4m3":
        words = by_word.astype(ml_dtypes.float8_e4m3fn).view(np.uint8)
    else:
        c = by_word.astype(ml_dtypes.float4_e2m1fn).view(np.uint8) & 0xF
        words = (c[..., 0::2] | (c[..., 1::2] << 4)).reshape(k // 512, 128, 2 * n)
    return np.ascontiguousarray(words), np.ascontiguousarray(byte.astype(np.uint8).reshape(k // 512, 16, n))


def unpack_weight(words, scales, fmt):
    g, _, n = scales.shape
    words = np.ascontiguousarray(words).reshape(g, 128, n, -1)
    if fmt == "e4m3":
        vals = words.view(ml_dtypes.float8_e4m3fn).astype(np.float64)
    else:
        nib = np.empty((g, 128, n, 4), np.uint8)
        nib[..., 0::2] = words & 0xF
        nib[..., 1::2] = words >> 4
        vals = E2M1[nib]
    vals = vals * np.repeat(np.exp2(scales.astype(np.float64) - 127.0), 8, axis=1)[..., None]
    return vals.transpose(0, 1, 3, 2).reshape(g * 512, n)


def gelu(v):
    return 0.5 * v * (1.0 + np.tanh(np.sqrt(2.0 / np.pi) * (v + 0.044715 * v**3)))


def bf(x):
    return np.asarray(x, np.float32).astype(ml_dtypes.bfloat16)


def planes(Y):
    n, m = Y.shape
    b = f64(bf(Y)).reshape(n // 32, 32, m)
    amax = np.abs(b).max(1)
    byte = np.clip(np.where(amax > 0, np.frexp(amax)[1] - 1 + 127 - 7, 1), 1, 254)
    codes = (b * np.exp2(127.0 - byte)[:, None, :]).reshape(n, m).astype(np.float32).astype(ml_dtypes.float8_e4m3fn).view(np.uint8)
    words = codes.reshape(n // 512, 128, 4, m).transpose(0, 1, 3, 2)
    return np.ascontiguousarray(words), np.ascontiguousarray(byte.astype(np.uint8).reshape(n // 512, 16, m))


T, S, P, K, H = 2048, 1024, 512, 1536, 1024

def setup_inputs():
    n = np.random.standard_normal
    s = mx_kscale(K)[:, None]
    u = mx_kscale(H)[:, None]
    tab_words, tab_scales = pack_weight(n((K, T)) * s, "e4m3")
    w1 = 0.8 * n((K, H)) / np.sqrt(K) / s
    w4_words, w4_scales = pack_weight(n((H, H)) / np.sqrt(H) / u, "e2m1")
    return {
        "tab_words": tab_words, "tab_scales": tab_scales,
        "offs": striped(np.random.permutation(T)[:S]),
        "pos1": striped(np.random.permutation(S)[:P]),
        "pos2": striped(np.random.permutation(S)[:P]),
        "w1": w1.astype(np.float32),
        "temp": np.random.uniform(0.4, 1.6, H).astype(np.float32),
        "gain": (np.random.uniform(3.0, 5.0, H) * u[:, 0]).astype(np.float32),
        "w4_words": w4_words, "w4_scales": w4_scales,
        "amp": np.exp(0.8 * n(H)).astype(np.float32),
    }

def reference(tab_words, tab_scales, offs, pos1, pos2, w1, temp, gain, w4_words, w4_scales, amp):
    v = unpack_weight(tab_words, tab_scales, "e4m3")[:, unstriped(offs)]
    h = mxq(f64(w1), 0, "e4m3").T @ v
    top = h.max(axis=1)
    a = np.exp(f64(temp)[:, None] * (h[:, unstriped(pos1)] - top[:, None]))
    c = h[:, unstriped(pos2)]
    x = a * c * f64(gain)[:, None]
    w4 = unpack_weight(w4_words, w4_scales, "e2m1")
    corr = w4.T @ mxq(x, 0, "e4m3")
    y = f64(amp)[:, None] * (corr + c)
    words, scales = planes(y)
    return y, words, scales

from contextlib import ExitStack

import concourse.mybir as mybir

T, S, PICK, K, H = 2048, 1024, 512, 1536, 1024
FLOPS = 2 * K * H * S + 2 * H * H * PICK

F32 = mybir.dt.float32
BF16 = mybir.dt.bfloat16
I32 = mybir.dt.int32
U32 = mybir.dt.uint32
U16 = mybir.dt.uint16
U8 = mybir.dt.uint8
FP8X4 = mybir.dt.float8_e4m3fn_x4
FP4X4 = mybir.dt.float4_e2m1fn_x4
ALU = mybir.AluOpType
ACT = mybir.ActivationFunctionType

P = 128
PACK = 4
GROUP = P * PACK
K_PASSES = K // GROUP
ROW_GROUPS = H // GROUP
BANK = 512
HALF = PICK // 2
LINE = 4


def tile_list_bead_profile_features_kernel(
    tc, tab_words, tab_scales, offs, pos1, pos2, w1, temp, gain, w4_words, w4_scales, amp, out_0, out_1, out_2
):
    nc = tc.nc
    with ExitStack() as ctx:
        keep = ctx.enter_context(tc.tile_pool(name="keep", bufs=1))
        ring = ctx.enter_context(tc.tile_pool(name="ring", bufs=1))
        psum = ctx.enter_context(tc.psum_pool(name="psum", bufs=8))

        offs_sb = keep.tile([P, S // 16], U16, name="offs_sb")
        pos1_sb = keep.tile([P, PICK // 16], U16, name="pos1_sb")
        pos2_sb = keep.tile([P, PICK // 16], U16, name="pos2_sb")
        temp_sb = keep.tile([P, ROW_GROUPS, PACK], F32, name="temp_sb")
        gain_sb = keep.tile([P, ROW_GROUPS, PACK], F32, name="gain_sb")
        amp_sb = keep.tile([P, ROW_GROUPS, PACK], F32, name="amp_sb")
        neg_temp = keep.tile([P, ROW_GROUPS, PACK], F32, name="neg_temp")
        look_bias = keep.tile([P, ROW_GROUPS, PACK], F32, name="look_bias")
        bank_max = keep.tile([P, ROW_GROUPS, PACK, 2], F32, name="bank_max")
        tab_w = [keep.tile([P, T], U32, name="tab_w%d" % a) for a in range(K_PASSES)]
        tab_s = keep.tile([P, T], U8, name="tab_s")
        v_w = [keep.tile([P, S], U32, name="v_w%d" % a, align_bytes=64) for a in range(K_PASSES)]
        v_s = keep.tile([P, S], U8, name="v_s", align_bytes=64)
        w4_raw_w = keep.tile([P, ROW_GROUPS, 2 * H], U8, name="w4_raw_w")
        w4_raw_s = keep.tile([P, ROW_GROUPS, H], U8, name="w4_raw_s")
        w4_w = keep.tile([P, ROW_GROUPS, 2 * H], U8, name="w4_w", align_bytes=64)
        w4_s = keep.tile([P, ROW_GROUPS, H], U8, name="w4_s", align_bytes=64)
        w1_codes = {}
        w1_scales = {}
        for b in range(ROW_GROUPS):
            for a in range(K_PASSES):
                w1_codes[b, a] = keep.tile([P, GROUP], U32, name="w1c%d%d" % (b, a), align_bytes=64)
                w1_scales[b, a] = keep.tile([P, GROUP], U8, name="w1s%d%d" % (b, a), align_bytes=64)
        x_rows = [keep.tile([P, 2, PACK, HALF], BF16, name="x_rows%d" % b) for b in range(ROW_GROUPS)]
        y = [keep.tile([P, 2, PACK, HALF], F32, name="y%d" % g) for g in range(ROW_GROUPS)]
        x_codes = {}
        x_scales = {}
        y_codes = {}
        for b in range(ROW_GROUPS):
            for half in range(2):
                x_codes[b, half] = keep.tile([P, HALF], U32, name="xc%d%d" % (b, half), align_bytes=64)
                x_scales[b, half] = keep.tile([P, HALF], U8, name="xs%d%d" % (b, half), align_bytes=64)
                y_codes[b, half] = keep.tile([P, HALF], U32, name="yc%d%d" % (b, half), align_bytes=64)
        y_scales = keep.tile([P, ROW_GROUPS, PICK], U8, name="y_scales", align_bytes=64)

        nc.vector.memset(tab_s[:].bitcast(I32), 0)
        nc.vector.memset(w4_raw_s[:].rearrange("p a c -> p (a c)").bitcast(I32), 0)
        for q in range(4):
            nc.gpsimd.dma_start(
                out=tab_s[32 * q : 32 * q + 4 * K_PASSES, :].bitcast(I32),
                in_=tab_scales[:, 4 * q : 4 * q + 4, :].bitcast(I32),
            )

        w1_raw = {}

        def load_w1(b, a, part):
            raw = ring.tile([P, PACK, GROUP // 2], F32, name="w1_raw", bufs=12)
            c0 = GROUP * b + part * (GROUP // 2)
            rows = w1[GROUP * a : GROUP * (a + 1), c0 : c0 + GROUP // 2]
            nc.sync.dma_start(out=raw[:], in_=rows.rearrange("(p j) c -> p j c", j=PACK))
            w1_raw[b, a, part] = raw

        nc.sync.dma_start(offs_sb[:], offs)
        for a in range(K_PASSES):
            nc.sync.dma_start(out=tab_w[a][:].bitcast(I32), in_=tab_words[a].rearrange("p n t -> p (n t)").bitcast(I32))
            load_w1(0, a, 0)
            load_w1(0, a, 1)
            if a == 0:
                for q in range(4):
                    nc.sync.dma_start(
                        out=w4_raw_s[32 * q : 32 * q + 4, :, :].bitcast(I32),
                        in_=w4_scales[:, 4 * q : 4 * q + 4, :].rearrange("a r c -> r a c").bitcast(I32),
                    )
            if a == 1:
                nc.sync.dma_start(pos1_sb[:], pos1)
                nc.sync.dma_start(pos2_sb[:], pos2)
                for vec, dst in ((temp, temp_sb), (gain, gain_sb), (amp, amp_sb)):
                    nc.sync.dma_start(out=dst[:], in_=vec.rearrange("(b p t) -> p b t", p=P, t=PACK))

        w1_bf = {}

        def round_w1(b, a, part, engine):
            if part == 0:
                w1_bf[b, a] = ring.tile([P, PACK, P, PACK], BF16, name="w1_bf", bufs=3, align_bytes=64)
            dst = w1_bf[b, a][:, :, part * (P // 2) : (part + 1) * (P // 2), :].rearrange("p t m j -> p m j t")
            src = w1_raw[b, a, part][:].rearrange("p j (m t) -> p m j t", t=PACK)
            if engine == "vector":
                nc.vector.tensor_copy(out=dst, in_=src)
            else:
                nc.scalar.copy(out=dst, in_=src)

        def quantize_w1(b, a, t0, t1):
            nc.vector.quantize_mx(
                out=w1_codes[b, a][:, P * t0 : P * t1].bitcast(FP8X4),
                scales=w1_scales[b, a][:, P * t0 : P * t1],
                in_=w1_bf[b, a][:, t0:t1, :, :].rearrange("p t m j -> p (t m j)"),
            )

        h_banks = {}

        def first_product(b, t, a):
            for side in range(2):
                if a == 0:
                    h_banks[b, t, side] = psum.tile([P, BANK], F32, name="bank", tag="bank")
                cols = slice(BANK * side, BANK * (side + 1))
                nc.tensor.matmul_mx(
                    out=h_banks[b, t, side][:],
                    lhsT=w1_codes[b, a][:, P * t : P * (t + 1)].bitcast(FP8X4),
                    lhsT_scale=w1_scales[b, a][:, P * t : P * (t + 1)],
                    rhs=v_w[a][:, cols].bitcast(FP8X4),
                    rhs_scale=v_s[4 * a : P, cols],
                    start=(a == 0),
                    stop=(a == K_PASSES - 1),
                )

        for a in range(K_PASSES):
            nc.vector.tensor_copy(v_w[a][:], tab_w[a][:].indirect(offs_sb[:]))
            if a == 0:
                nc.vector.tensor_copy(v_s[:], tab_s[:].indirect(offs_sb[:]))
            if a == 2:
                nc.vector.tensor_scalar(out=neg_temp[:], in0=temp_sb[:], scalar1=-1.0, scalar2=None, op0=ALU.mult)
            if a == 1:
                nc.vector.tensor_copy(
                    out=w4_s[:].rearrange("p a (g t q) -> p (a g) q t", t=PACK, q=P),
                    in_=w4_raw_s[:].rearrange("p a (g q t) -> p (a g) q t", t=PACK, q=P),
                )
            last = a == K_PASSES - 1
            round_w1(0, a, 0, "scalar")
            round_w1(0, a, 1, "vector" if last else "scalar")
            if last:
                for t in range(PACK):
                    quantize_w1(0, a, t, t + 1)
                    first_product(0, t, a)
            else:
                quantize_w1(0, a, 0, PACK)
                for t in range(PACK):
                    first_product(0, t, a)

        for a in range(K_PASSES):
            load_w1(1, a, 0)
            load_w1(1, a, 1)
        nc.sync.dma_start(out=w4_raw_w[:].bitcast(I32), in_=w4_words.rearrange("a p c -> p a c").bitcast(I32))

        h_rows = {}
        look = {}
        ctrl = {}

        def leave_psum(b, t):
            h_rows[b, t] = ring.tile([P, S], F32, name="h_rows", bufs=5)
            for side in range(2):
                nc.vector.tensor_scalar(
                    out=h_rows[b, t][:, BANK * side : BANK * (side + 1)],
                    in0=h_banks[b, t, side][:],
                    scalar1=1.0,
                    scalar2=None,
                    op0=ALU.mult,
                    op1=ALU.max,
                    accum_out=bank_max[:, b, t, side : side + 1],
                )
            nc.vector.tensor_scalar(
                out=look_bias[:, b, t : t + 1],
                in0=bank_max[:, b, t, 0:1],
                scalar1=bank_max[:, b, t, 1:2],
                scalar2=neg_temp[:, b, t : t + 1],
                op0=ALU.max,
                op1=ALU.mult,
            )
            look[b, t] = ring.tile([P, PICK], F32, name="look", bufs=5)
            nc.scalar.activation(
                out=look[b, t][:],
                in_=h_rows[b, t][:].indirect(pos1_sb[:]),
                func=ACT.Exp,
                bias=look_bias[:, b, t : t + 1],
                scale=temp_sb[:, b, t : t + 1],
            )

        def pick(b, t, h0, h1):
            width = HALF * (h1 - h0)
            ctrl[b, t, h0] = ring.tile([P, width], F32, name="ctrl", bufs=4)
            nc.vector.tensor_copy(
                ctrl[b, t, h0][:], h_rows[b, t][:].indirect(pos2_sb[:, HALF * h0 // 16 : HALF * h1 // 16])
            )
            nc.scalar.activation(
                out=y[b][:, h0:h1, t, :],
                in_=ctrl[b, t, h0][:].rearrange("p (h m) -> p h m", m=HALF),
                func=ACT.Copy,
                scale=amp_sb[:, b, t : t + 1],
            )

        def combine(b, t, h0, h1):
            nc.vector.scalar_tensor_tensor(
                out=x_rows[b][:, h0:h1, t, :],
                in0=look[b, t][:, HALF * h0 : HALF * h1].rearrange("p (h m) -> p h m", m=HALF),
                scalar=gain_sb[:, b, t : t + 1],
                in1=ctrl[b, t, h0][:].rearrange("p (h m) -> p h m", m=HALF),
                op0=ALU.mult,
                op1=ALU.mult,
            )

        woven = {}

        def weave(key, rows, engine):
            woven[key] = ring.tile([P, HALF, PACK], BF16, name="woven", bufs=3, align_bytes=64)
            dst = woven[key][:].rearrange("p (c i) t -> p c t i", i=LINE)
            src = rows.rearrange("p t (c i) -> p c t i", i=LINE)
            if engine == "vector":
                nc.vector.tensor_copy(out=dst, in_=src)
            else:
                nc.scalar.copy(out=dst, in_=src)

        def quantize_x(b, half):
            nc.vector.quantize_mx(
                out=x_codes[b, half][:].bitcast(FP8X4),
                scales=x_scales[b, half][:],
                in_=woven["x", b, half][:].rearrange("p m t -> p (m t)"),
            )

        corr = {}

        def second_product(g, half):
            for t in range(PACK):
                if t % 2 == 0:
                    bank = psum.tile([P, 2, HALF], F32, name="bank", tag="bank")
                corr[g, half, t] = bank[:, t % 2, :]
                c0 = GROUP * g + P * t
                for b in range(ROW_GROUPS):
                    nc.tensor.matmul_mx(
                        out=corr[g, half, t],
                        lhsT=w4_w[:, b, 2 * c0 : 2 * (c0 + P)].bitcast(FP4X4),
                        lhsT_scale=w4_s[:, b, c0 : c0 + P],
                        rhs=x_codes[b, half][:].bitcast(FP8X4),
                        rhs_scale=x_scales[b, half][:],
                        start=(b == 0),
                        stop=(b == ROW_GROUPS - 1),
                    )

        def finish_rows(g, half):
            for t in range(PACK):
                nc.vector.scalar_tensor_tensor(
                    out=y[g][:, half, t, :],
                    in0=corr[g, half, t],
                    scalar=amp_sb[:, g, t : t + 1],
                    in1=y[g][:, half, t, :],
                    op0=ALU.mult,
                    op1=ALU.add,
                )
            dst = out_0[GROUP * g : GROUP * (g + 1), HALF * half : HALF * (half + 1)]
            nc.sync.dma_start(out=dst.rearrange("(p t) m -> p t m", t=PACK), in_=y[g][:, half, :, :])

        def quantize_y(g, half):
            nc.vector.quantize_mx(
                out=y_codes[g, half][:].bitcast(FP8X4),
                scales=y_scales[:, g, HALF * half : HALF * (half + 1)],
                in_=woven["y", g, half][:].rearrange("p m t -> p (m t)"),
            )
            dst = out_1[g].rearrange("p m t -> p (m t)").bitcast(I32)[:, HALF * half : HALF * (half + 1)]
            nc.sync.dma_start(out=dst, in_=y_codes[g, half][:].bitcast(I32))

        for t in range(PACK):
            leave_psum(0, t)
            if t > 0:
                combine(0, t - 1, 0, 2)
            pick(0, t, 0, 2)
            if t < K_PASSES:
                round_w1(1, t, 0, "scalar")
                round_w1(1, t, 1, "scalar")
            if t > 0:
                quantize_w1(1, t - 1, 0, PACK)
        for t in range(PACK):
            for a in range(K_PASSES):
                first_product(1, t, a)
        combine(0, PACK - 1, 0, 2)
        for half in range(2):
            weave(("x", 0, half), x_rows[0][:, half, :, :], "scalar")
        nc.scalar.copy(
            out=w4_w[:].bitcast(U16).rearrange("p a (g t q) -> p (a g) q t", t=PACK, q=P),
            in_=w4_raw_w[:].bitcast(U16).rearrange("p a (g q t) -> p (a g) q t", t=PACK, q=P),
        )

        for t in range(PACK):
            leave_psum(1, t)
            if t > 0:
                combine(1, t - 1, 0, 1)
            pick(1, t, 0, 1)
            if t in (1, 2):
                quantize_x(0, t - 1)
        pick(1, 0, 1, 2)
        combine(1, PACK - 1, 0, 1)
        weave(("x", 1, 0), x_rows[1][:, 0, :, :], "scalar")
        for t in range(1, PACK):
            pick(1, t, 1, 2)
            combine(1, t - 1, 1, 2)
            if t == 2:
                quantize_x(1, 0)
                second_product(0, 0)
                second_product(1, 0)
        combine(1, PACK - 1, 1, 2)
        weave(("x", 1, 1), x_rows[1][:, 1, :, :], "scalar")

        finish_rows(0, 0)
        weave(("y", 0, 0), y[0][:, 0, :, :], "scalar")
        quantize_x(1, 1)
        second_product(0, 1)
        second_product(1, 1)
        finish_rows(1, 0)
        weave(("y", 1, 0), y[1][:, 0, :, :], "scalar")
        quantize_y(0, 0)
        finish_rows(0, 1)
        weave(("y", 0, 1), y[0][:, 1, :, :], "scalar")
        quantize_y(1, 0)
        finish_rows(1, 1)
        quantize_y(0, 1)
        weave(("y", 1, 1), y[1][:, 1, :, :], "vector")
        quantize_y(1, 1)
        for q in range(4):
            nc.sync.dma_start(
                out=out_2[:, 4 * q : 4 * q + 4, :].rearrange("g r m -> r g m").bitcast(I32),
                in_=y_scales[32 * q : 32 * q + 4, :, :].bitcast(I32),
            )
